import numpy as np
import ml_dtypes


def mxq(x, axis, fmt="e4m3"):
    dtype, down = {"e4m3": (ml_dtypes.float8_e4m3fn, 7), "e5m2": (ml_dtypes.float8_e5m2, 14)}[fmt]
    v = np.moveaxis(np.asarray(x, np.float32).astype(ml_dtypes.bfloat16).astype(np.float64), axis, -1)
    blocks = v.reshape(v.shape[:-1] + (-1, 32))
    amax = np.abs(blocks).max(-1, keepdims=True)
    byte = np.maximum(np.where(amax > 0, np.frexp(amax)[1] - 1 + 127, 0) - down, 1)
    scale = np.exp2(byte - 127.0)
    codes = (blocks / scale).astype(np.float32).astype(dtype).astype(np.float64)
    return np.moveaxis((codes * scale).reshape(v.shape), -1, axis)


WIDE = False


def mx_kscale(k):
    if not WIDE:
        return np.ones(k)
    levels = np.array([10, -10, 5, -5, 0])
    if k % 512:
        return np.exp2(np.random.permutation(np.resize(levels, k // 32))).repeat(32)
    a = np.empty((k // 512, 16))
    for p in range(k // 512):
        a[p, :8] = np.random.permutation(np.resize(levels, 8))
        for g in range(8):
            far = levels[np.abs(levels - a[p, g]) >= 10]
            a[p, g + 8] = far[np.random.randint(len(far))]
    return np.exp2(a.ravel()).repeat(32)


def f64(x):
    return np.asarray(x).astype(np.float64)


def striped(idx):
    return np.tile(idx.reshape(-1, 16).T, (8, 1)).astype(np.uint16)


def unstriped(offs):
    return offs[:16].T.reshape(-1).astype(np.int64)


E2M1 = np.array([0.0, 0.5, 1.0, 1.5, 2.0, 3.0, 4.0, 6.0, -0.0, -0.5, -1.0, -1.5, -2.0, -3.0, -4.0, -6.0])


def pack_weight(w, fmt):
    k, n = w.shape
    w = f64(np.asarray(w, np.float32).astype(ml_dtypes.bfloat16)).reshape(k // 32, 32, n)
    amax = np.abs(w).max(1)
    if fmt == "e4m3":
        byte = np.frexp(amax)[1] - 1 + 127 - 7
    else:
        mant, ex = np.frexp(amax / 6.0)
        byte = np.where(mant > 0.5, ex, ex - 1) + 127
    byte = np.clip(np.where(amax > 0, byte, 1), 1, 254)
    scaled = (w * np.exp2(127.0 - byte)[:, None, :]).reshape(k, n).astype(np.float32)
    by_word = np.ascontiguousarray(scaled.reshape(k // 512, 128, 4, n).transpose(0, 1, 3, 2))
    if fmt == "e4m3":
        words = by_word.astype(ml_dtypes.float8_e4m3fn).view(np.uint8)
    else:
        c = by_word.astype(ml_dtypes.float4_e2m1fn).view(np.uint8) & 0xF
        words = (c[..., 0::2] | (c[..., 1::2] << 4)).reshape(k // 512, 128, 2 * n)
    return np.ascontiguousarray(words), np.ascontiguousarray(byte.astype(np.uint8).reshape(k // 512, 16, n))


def unpack_weight(words, scales, fmt):
    g, _, n = scales.shape
    words = np.ascontiguousarray(words).reshape(g, 128, n, -1)
    if fmt == "e4m3":
        vals = words.view(ml_dtypes.float8_e4m3fn).astype(np.float64)
    else:
        nib = np.empty((g, 128, n, 4), np.uint8)
        nib[..., 0::2] = words & 0xF
        nib[..., 1::2] = words >> 4
        vals = E2M1[nib]
    vals = vals * np.repeat(np.exp2(scales.astype(np.float64) - 127.0), 8, axis=1)[..., None]
    return vals.transpose(0, 1, 3, 2).reshape(g * 512, n)


def gelu(v):
    return 0.5 * v * (1.0 + np.tanh(np.sqrt(2.0 / np.pi) * (v + 0.044715 * v**3)))


def striped8(idx):
    return np.concatenate([v.reshape(-1, 16).T for v in idx]).astype(np.uint16)


def unstriped8(offs):
    return np.stack([offs[16 * g:16 * g + 16].T.reshape(-1) for g in range(8)]).astype(np.int64)


def heads(h, wgt, idx8):
    r = np.arange(h.shape[0])
    return wgt[r // 4 % 128] * h[r[:, None], idx8[r % 512 // 64]]


def put_heads(h, wgs, idx8, t2):
    r = np.arange(h.shape[0])
    page = np.zeros((h.shape[0], t2))
    page[r[:, None], idx8[r % 512 // 64]] = wgs[r // 4 % 128] * h
    return page


K, T, S, T2, P, H, N = 512, 4096, 1024, 2048, 1024, 1024, 768

def setup_inputs():
    n = np.random.standard_normal
    s = mx_kscale(K)[:, None]
    u = mx_kscale(H)[:, None]
    d = {}
    d["tab_words"], d["tab_scales"] = pack_weight(n((K, T)) * s, "e4m3")
    d["offs"] = striped(np.random.permutation(T)[:S])
    d["offs2"] = striped8(np.stack([np.random.permutation(T2)[:S] for _ in range(8)]))
    d["offs3"] = striped8(np.stack([np.random.permutation(T2)[:P] for _ in range(8)]))
    d["wgs"] = np.repeat(np.random.uniform(0.5, 2.0, (8, S)), 16, axis=0).astype(np.float32)
    d["wgt"] = np.repeat(np.random.uniform(0.5, 2.0, (8, P)), 16, axis=0).astype(np.float32)
    d["w1"] = (1.6 * n((K, H)) / s / K**0.5).astype(np.float32)
    d["w2_words"], d["w2_scales"] = pack_weight(0.13 * n((K, H)) / s / K**0.5, "e4m3")
    d["amp"] = np.random.uniform(0.15, 0.35, H).astype(np.float32)
    d["swell"] = np.random.uniform(-2.0, 0.3, (H, P)).astype(np.float32)
    d["lift"] = (np.exp(0.3 * n(H)) * u[:, 0]).astype(np.float32)
    d["w3_words"], d["w3_scales"] = pack_weight(n((H, N)) / u / H**0.5, "e2m1")
    return d

def reference(tab_words, tab_scales, offs, offs2, offs3, wgs, wgt, w1, w2_words, w2_scales, amp, swell, lift, w3_words, w3_scales):
    v = unpack_weight(tab_words, tab_scales, "e4m3")[:, unstriped(offs)]
    w2 = unpack_weight(w2_words, w2_scales, "e4m3")
    w3 = unpack_weight(w3_words, w3_scales, "e2m1")
    bend = f64(amp)[:, None] * np.tanh(mxq(f64(w1), 0, "e4m3").T @ v)
    h = np.abs(bend - (w2.T @ v))
    page = put_heads(h, f64(wgs), unstriped8(offs2), T2)
    x = heads(page, f64(wgt), unstriped8(offs3))
    z = f64(lift)[:, None] * np.sin(x + f64(swell))
    return w3.T @ mxq(z, 0, "e4m3")

@@ -1,0 +1,329 @@
+import math
+from contextlib import ExitStack
+
+import concourse.mybir as mybir
+from concourse.masks import make_identity
+
+K, T, S, T2, M, H, N = 512, 4096, 1024, 2048, 1024, 1024, 768
+FLOPS = 2 * (2 * K * H * S + H * N * M)
+
+F32 = mybir.dt.float32
+BF16 = mybir.dt.bfloat16
+I32 = mybir.dt.int32
+U32 = mybir.dt.uint32
+U16 = mybir.dt.uint16
+U8 = mybir.dt.uint8
+FP8X4 = mybir.dt.float8_e4m3fn_x4
+FP4X4 = mybir.dt.float4_e2m1fn_x4
+ACT = mybir.ActivationFunctionType
+ALU = mybir.AluOpType
+
+P = 128
+PACK = 4
+BANK = 512
+TILES = H // P
+TURN = 2.0 * math.pi
+ROUNDER = 1.5 * 2.0**23
+CHUNK = 256
+EARLY = {6: [0, 1], 7: [2], 8: [3]}
+WOVEN_BY_SCALAR = []
+ENDS = 3
+DEPTH = 1
+ON_VECTOR = [(2, 2), (3, 1), (4, 0), (4, 2)]
+WIDTHS = [256, 256, 256, 128, 128]
+
+
+def tile_list_skirt_flutter_features_kernel(
+    tc, tab_words, tab_scales, offs, offs2, offs3, wgs, wgt, w1, w2_words, w2_scales, amp, swell, lift, w3_words, w3_scales, out
+):
+    nc = tc.nc
+    with ExitStack() as ctx:
+        keep = ctx.enter_context(tc.tile_pool(name="keep", bufs=1))
+        ring = ctx.enter_context(tc.tile_pool(name="ring", bufs=2))
+        psum = ctx.enter_context(tc.psum_pool(name="psum", bufs=1))
+        banks = [psum.tile([P, BANK], F32, name="bank%d" % n) for n in range(8)]
+
+        def held(shape, dtype, name):
+            return keep.tile(shape, dtype, name=name, align_bytes=64)
+
+        idx = held([P, S // 16], U16, "idx")
+        idx2 = held([P, S // 16], U16, "idx2")
+        idx3 = held([P, M // 16], U16, "idx3")
+        tab_s = held([P, T], U8, "tab_s")
+        w2_raw_w = keep.tile([P, H], I32, name="w2_raw_w", tag="gains")
+        w2_raw_s = keep.tile([P, H], U8, name="w2_raw_s", tag="rows")
+        w2_w = held([P, H], I32, "w2_w")
+        w2_s = held([P, H], U8, "w2_s")
+        w1_bf = [keep.tile([P, PACK * BANK], BF16, name="w1_bf%d" % b, tag="w1_bf%d" % b, align_bytes=64) for b in range(2)]
+        w1_w = [held([P, BANK], I32, "w1_w%d" % b) for b in range(2)]
+        w1_s = [held([P, BANK], U8, "w1_s%d" % b) for b in range(2)]
+        v_w = [held([P, BANK], I32, "v_w%d" % u) for u in range(2)]
+        v_s = [held([P, BANK], U8, "v_s%d" % u) for u in range(2)]
+        page = held([P, T2], F32, "page")
+        ident = held([P, P], F32, "ident")
+        zero_in = keep.tile([P, 1], F32, name="zero_in", tag="tab_w", align_bytes=64)
+        zero = held([P, 1], F32, "zero")
+        tx = [held([P, S], F32, "tx%d" % u) for u in range(2)]
+        hw = [held([P, S], F32, "hw%d" % u) for u in range(2)]
+        wave = held([P, M], F32, "wave")
+        xm = held([P, M], F32, "xm")
+        z_rows = [held([P, PACK, M], BF16, "z_rows%d" % b) for b in range(2)]
+        z_w = [held([P, M], I32, "z_w%d" % b) for b in range(2)]
+        z_s = [held([P, M], U8, "z_s%d" % b) for b in range(2)]
+        swell_rows = swell.rearrange("(b p i) m -> b i p m", p=P, i=PACK)
+        w1_rows = w1.rearrange("(p j) c -> p j c", j=PACK)
+
+        nc.vector.memset(tab_s[:].bitcast(I32), 0)
+        nc.vector.memset(w2_raw_s[:].bitcast(I32), 0)
+        nc.gpsimd.memset(zero_in[:], 0.0)
+        nc.scalar.activation(zero[:], zero_in[:], ACT.Silu)
+        nc.sync.dma_start(idx[:], offs)
+        nc.sync.dma_start(idx2[:], offs2)
+        nc.sync.dma_start(idx3[:], offs3)
+        nc.sync.dma_start(w2_raw_w[:], w2_words[0].rearrange("p c i -> p (c i)").bitcast(I32))
+        w1_raw = [None, None]
+        w1_raw[0] = keep.tile([P, PACK, BANK], F32, name="w1_raw", tag="w1_raw", align_bytes=64)
+        nc.sync.dma_start(w1_raw[0][:], w1_rows[:, :, 0:BANK])
+        tab_w = keep.tile([P, T], I32, name="tab_w", tag="tab_w", align_bytes=64)
+        nc.sync.dma_start(tab_w[:], tab_words[0].rearrange("p t i -> p (t i)").bitcast(I32))
+        for q in range(4):
+            nc.scalar.dma_start(tab_s[32 * q : 32 * q + 4, :].bitcast(I32), tab_scales[0, 4 * q : 4 * q + 4, :].bitcast(I32))
+        for q in range(4):
+            nc.scalar.dma_start(w2_raw_s[32 * q : 32 * q + 4, :].bitcast(I32), w2_scales[0, 4 * q : 4 * q + 4, :].bitcast(I32))
+        nc.vector.memset(page[:], 0.0)
+        make_identity(nc, ident[:])
+
+        def cast_w1(engine_copy, b, i):
+            engine_copy(
+                w1_bf[b][:, BANK * i : BANK * (i + 1)].rearrange("p (m j) -> p m j", j=PACK),
+                w1_raw[b][:].rearrange("p j (m i) -> p i m j", i=PACK)[:, i],
+            )
+
+        def quantize_w1(b):
+            nc.vector.quantize_mx(out=w1_w[b][:].bitcast(FP8X4), scales=w1_s[b][:], in_=w1_bf[b][:])
+
+        nc.vector.tensor_copy(
+            w2_w[:].rearrange("p (b i m) -> p b i m", b=2, i=PACK), w2_raw_w[:].rearrange("p (b m i) -> p b i m", b=2, i=PACK)
+        )
+        nc.vector.tensor_copy(
+            w2_s[:].rearrange("p (b i m) -> p b i m", b=2, i=PACK), w2_raw_s[:].rearrange("p (b m i) -> p b i m", b=2, i=PACK)
+        )
+        gains = keep.tile([P, S + M + 2 * TILES], F32, name="gains", tag="gains")
+        wgs_t = gains[:, 0:S]
+        wgt_t = gains[:, S : S + M]
+        amp_t = gains[:, S + M : S + M + TILES]
+        lift_t = gains[:, S + M + TILES : S + M + 2 * TILES]
+        nc.sync.dma_start(amp_t.rearrange("p (b i) -> p b i", b=2), amp.rearrange("(b p i) -> p b i", p=P, i=PACK))
+        nc.sync.dma_start(wgs_t, wgs)
+        nc.sync.dma_start(wgt_t, wgt)
+        nc.sync.dma_start(lift_t.rearrange("p (b i) -> p b i", b=2), lift.rearrange("(b p i) -> p b i", p=P, i=PACK))
+        for i in range(PACK):
+            cast_w1(nc.vector.tensor_copy, 0, i)
+        quantize_w1(0)
+        w1_raw[1] = keep.tile([P, PACK, BANK], F32, name="w1_raw", tag="w1_raw", align_bytes=64)
+        nc.sync.dma_start(w1_raw[1][:], w1_rows[:, :, BANK : 2 * BANK])
+        for u in range(2):
+            part = idx[:, 32 * u : 32 * (u + 1)]
+            nc.vector.tensor_copy(v_w[u][:].bitcast(U32), tab_w[:].bitcast(U32).indirect(part))
+            nc.vector.tensor_copy(v_s[u][:], tab_s[:].indirect(part))
+
+        def half(u):
+            return slice(BANK * u, BANK * (u + 1))
+
+        linear = {}
+
+        def products(t):
+            b, i = divmod(t, PACK)
+            cols = slice(P * i, P * (i + 1))
+            cols2 = slice(P * t, P * (t + 1))
+            for u in range(2):
+                bent = banks[u]
+                nc.tensor.matmul_mx(
+                    out=bent[:], lhsT=w1_w[b][:, cols].bitcast(FP8X4), lhsT_scale=w1_s[b][:, cols],
+                    rhs=v_w[u][:].bitcast(FP8X4), rhs_scale=v_s[u][:], start=True, stop=True,
+                )
+                lin = banks[2 + 2 * (t % 2) + u]
+                nc.tensor.matmul_mx(
+                    out=lin[:], lhsT=w2_w[:, cols2].bitcast(FP8X4), lhsT_scale=w2_s[:, cols2],
+                    rhs=v_w[u][:].bitcast(FP8X4), rhs_scale=v_s[u][:], start=True, stop=True,
+                )
+                linear[t, u] = lin
+                nc.scalar.activation(tx[t % 2][:, half(u)], bent[:], ACT.Tanh, bias=zero[:])
+
+        h_of = {}
+
+        def difference(t):
+            b, i = divmod(t, PACK)
+            diff = tx[(t + 1) % 2]
+            h = hw[t % 2]
+            for u in range(2):
+                nc.vector.scalar_tensor_tensor(
+                    diff[:, half(u)], tx[t % 2][:, half(u)], amp_t[:, t : t + 1], linear[t, u][:], ALU.mult, ALU.subtract
+                )
+                if t == 0:
+                    nc.scalar.activation(h[:, half(u)], diff[:, half(u)], ACT.Abs)
+            if t > 0:
+                nc.scalar.activation(h[:], diff[:], ACT.Abs)
+            h_of[t] = h
+
+        def put(t):
+            if t == 0:
+                for u in range(2):
+                    nc.vector.tensor_tensor(
+                        page[:].indirect(idx2[:, 32 * u : 32 * (u + 1)]), h_of[t][:, half(u)], wgs_t[:, half(u)], ALU.mult
+                    )
+            else:
+                nc.vector.tensor_tensor(page[:].indirect(idx2[:]), h_of[t][:], wgs_t, ALU.mult)
+
+        def pick(t):
+            nc.vector.tensor_tensor(xm[:], page[:].indirect(idx3[:]), wgt_t, ALU.mult)
+
+        swell_of = {}
+
+        def load_swell(t):
+            rows = keep.tile([P, M], F32, name="swell_t", tag="rows")
+            nc.sync.dma_start(rows[:], swell_rows[t // PACK, t % PACK])
+            swell_of[t] = rows
+
+        def add_turned(bank, sources):
+            steps = [(src, c) for src in sources for c in range(BANK // P)]
+            for n, (src, c) in enumerate(steps):
+                nc.tensor.matmul(
+                    bank[:, P * c : P * (c + 1)], lhsT=src[:, P * c : P * (c + 1)], rhs=ident[:],
+                    is_transpose=True, start=(n == 0), stop=(n == len(steps) - 1),
+                )
+
+        def sine(t):
+            b, i = divmod(t, PACK)
+            x = xm
+            turns = tx[(t + 1) % 2]
+            minus = xm
+            pair = banks[2 + 2 * ((t + 1) % 2) :]
+            for u in range(2):
+                add_turned(pair[u], [x[:, half(u)], swell_of[t][:, half(u)]])
+            for u in range(2):
+                nc.scalar.activation(turns[:, half(u)], pair[u][:], ACT.Copy, scale=1.0 / TURN)
+                whole = keep.tile([P, BANK], U32, name="whole", tag="whole%d%d" % (t % 2, u), align_bytes=64)
+                nc.scalar.activation(whole[:], turns[:, half(u)], ACT.Copy, bias=ROUNDER)
+                nc.scalar.activation(minus[:, half(u)], whole[:], ACT.Copy, scale=-1.0, bias=ROUNDER)
+                add_turned(pair[u], [turns[:, half(u)], minus[:, half(u)]])
+            for u in range(2):
+                nc.scalar.activation(wave[:, half(u)], pair[u][:], ACT.Sin, scale=TURN)
+
+        def gain(t):
+            b, i = divmod(t, PACK)
+            nc.scalar.activation(z_rows[b][:, i, :], wave[:], ACT.Copy, scale=lift_t[:, t : t + 1])
+
+        def weave(engine_copy, b, cols, woven):
+            engine_copy(
+                woven.rearrange("p (g e i) -> p g i e", e=4, i=PACK),
+                z_rows[b][:, :, cols].rearrange("p i (g e) -> p g i e", e=4),
+            )
+            return woven
+
+        def quantize_z(b, cols, woven):
+            nc.vector.quantize_mx(out=z_w[b][:, cols].bitcast(FP8X4), scales=z_s[b][:, cols], in_=woven)
+
+        last = TILES - 1
+        load_swell(0)
+        products(0)
+        difference(0)
+        extras = {1: [0, 1, 2], 2: [3]}
+        swell_turns = held([P, M], F32, "swell_turns")
+        for t in range(1, TILES + 1):
+            if t < TILES:
+                products(t)
+            if t >= 2:
+                sine(t - 2)
+            if 2 <= t <= last:
+                load_swell(t - 1)
+            put(t - 1)
+            for u, c in enumerate(EARLY.get(t, [])):
+                cols = slice(CHUNK * c, CHUNK * (c + 1))
+                woven = keep.tile([P, CHUNK * PACK], BF16, name="woven", tag="whole%d%d" % (t % 2, u), align_bytes=64)
+                quantize_z(0, cols, weave(nc.scalar.copy, 0, cols, woven[:]))
+            if t < TILES:
+                difference(t)
+            if t >= 2:
+                gain(t - 2)
+            if t < TILES:
+                pick(t - 1)
+            if t == 1:
+                w3_w = keep.tile([P, 2, 2 * N], U8, name="w3_w", tag="w1_bf0", align_bytes=64)
+                nc.sync.dma_start(w3_w[:].bitcast(I32), w3_words.bitcast(I32).rearrange("b p c -> p b c"))
+            for i in extras.get(t, []):
+                cast_w1(nc.scalar.copy, 1, i)
+            if t == 2:
+                quantize_w1(1)
+                w3_s = keep.tile([P, 2 * N], U8, name="w3_s", tag="w1_raw", align_bytes=64)
+                nc.gpsimd.memset(w3_s[:].bitcast(I32), 0)
+                for q in range(4):
+                    nc.sync.dma_start(
+                        w3_s[32 * q : 32 * q + 4, :].bitcast(I32).rearrange("r (b c) -> r b c", b=2),
+                        w3_scales[:, 4 * q : 4 * q + 4, :].bitcast(I32).rearrange("b r c -> r b c"),
+                    )
+                swell_last = keep.tile([P, M], F32, name="swell_last", tag="w1_bf1", align_bytes=64)
+                nc.sync.dma_start(swell_last[:], swell_rows[1, PACK - 1])
+            if t == 3:
+                nc.scalar.activation(swell_turns[:], swell_last[:], ACT.Copy, scale=1.0 / TURN)
+
+        out_rows = out.rearrange("(g n p) m -> g p n m", p=P, n=2)
+
+        starts = [sum(WIDTHS[:c]) for c in range(len(WIDTHS))]
+        chunks = len(WIDTHS)
+        ends = [xm[:, half(0)], xm[:, half(1)], tx[1][:, half(0)], tx[1][:, half(1)]]
+        small = ctx.enter_context(tc.tile_pool(name="small", bufs=DEPTH))
+
+        def front(c):
+            width = WIDTHS[c]
+            cols = slice(starts[c], starts[c] + width)
+            x = ends[c % ENDS][:, 0:width]
+            turns = small.tile([P, width], F32, name="turns_end")
+            whole = small.tile([P, width], I32, name="whole_end")
+            rest = small.tile([P, width], F32, name="rest_end")
+            nc.vector.tensor_tensor(x, page[:].indirect(idx3[:, cols.start // 16 : cols.stop // 16]), wgt_t[:, cols], ALU.mult)
+            nc.vector.scalar_tensor_tensor(turns[:], x, 1.0 / TURN, swell_turns[:, cols], ALU.mult, ALU.add)
+            nc.vector.tensor_scalar(whole[:], turns[:], ROUNDER, None, ALU.add)
+            nc.vector.scalar_tensor_tensor(rest[:], whole[:], ROUNDER, turns[:], ALU.subtract, ALU.subtract)
+            nc.scalar.activation(wave[:, cols], rest[:], ACT.Sin, scale=-TURN)
+            nc.scalar.activation(z_rows[1][:, PACK - 1, cols], wave[:, cols], ACT.Copy, scale=lift_t[:, last : last + 1])
+
+        def middle(c):
+            cols = slice(starts[c], starts[c] + WIDTHS[c])
+            quantize_z(1, cols, weave(nc.scalar.copy if c in WOVEN_BY_SCALAR else nc.vector.tensor_copy, 1, cols, ends[c % ENDS][:, 0 : 2 * WIDTHS[c]].bitcast(BF16)))
+
+        out_banks = [2, 3, 4, 5, 0, 1, 6, 7]
+
+        def back(c):
+            width = WIDTHS[c]
+            cols = slice(starts[c], starts[c] + width)
+            for g in range(N // (2 * P)):
+                bank = out_banks[(3 * c + g) % 8]
+                acc = banks[bank][:, 0 : 2 * width].rearrange("p (n m) -> p n m", n=2)
+                passes = (1, 0) if 4 <= 3 * c + g < 8 else (0, 1)
+                steps = [(b, n, w) for b in passes for n in range(2) for w in range(width // P)]
+                for s, (b, n, w) in enumerate(steps):
+                    rows = 2 * g + n
+                    part = slice(cols.start + P * w, cols.start + P * (w + 1))
+                    nc.tensor.matmul_mx(
+                        out=acc[:, n, P * w : P * (w + 1)],
+                        lhsT=w3_w[:, b, 2 * P * rows : 2 * P * (rows + 1)].bitcast(FP4X4),
+                        lhsT_scale=w3_s[:, N * b + P * rows : N * b + P * (rows + 1)],
+                        rhs=z_w[b][:, part].bitcast(FP8X4),
+                        rhs_scale=z_s[b][:, part],
+                        start=(s == 0), stop=(s == len(steps) - 1),
+                    )
+                result = keep.tile([P, 2, width], F32, name="result%d_%d" % (c, g))
+                if (c, g) in ON_VECTOR:
+                    nc.vector.tensor_copy(result[:], acc)
+                else:
+                    nc.scalar.copy(result[:], acc)
+                nc.sync.dma_start(out_rows[g, :, :, cols], result[:])
+
+        for c in range(ENDS):
+            front(c)
+        for c in range(chunks):
+            middle(c)
+            if c + ENDS < chunks:
+                front(c + ENDS)
+            back(c)

@@ -29,7 +29,7 @@ EARLY = {6: [0, 1], 7: [2], 8: [3]}
 WOVEN_BY_SCALAR = []
 ENDS = 3
 DEPTH = 1
-ON_VECTOR = [(2, 2), (3, 1), (4, 0), (4, 2)]
+SHARED_FROM = 6
 WIDTHS = [256, 256, 256, 128, 128]
 
 
@@ -40,6 +40,7 @@ def tile_list_skirt_flutter_features_kernel(
     with ExitStack() as ctx:
         keep = ctx.enter_context(tc.tile_pool(name="keep", bufs=1))
         ring = ctx.enter_context(tc.tile_pool(name="ring", bufs=2))
+        early = ctx.enter_context(tc.tile_pool(name="early", bufs=1))
         psum = ctx.enter_context(tc.psum_pool(name="psum", bufs=1))
         banks = [psum.tile([P, BANK], F32, name="bank%d" % n) for n in range(8)]
 
@@ -49,19 +50,18 @@ def tile_list_skirt_flutter_features_kernel(
         idx = held([P, S // 16], U16, "idx")
         idx2 = held([P, S // 16], U16, "idx2")
         idx3 = held([P, M // 16], U16, "idx3")
+        tab_w = early.tile([P, T], I32, name="tab_w", offset=13 * S)
         tab_s = held([P, T], U8, "tab_s")
-        w2_raw_w = keep.tile([P, H], I32, name="w2_raw_w", tag="gains")
         w2_raw_s = keep.tile([P, H], U8, name="w2_raw_s", tag="rows")
         w2_w = held([P, H], I32, "w2_w")
         w2_s = held([P, H], U8, "w2_s")
-        w1_bf = [keep.tile([P, PACK * BANK], BF16, name="w1_bf%d" % b, tag="w1_bf%d" % b, align_bytes=64) for b in range(2)]
         w1_w = [held([P, BANK], I32, "w1_w%d" % b) for b in range(2)]
         w1_s = [held([P, BANK], U8, "w1_s%d" % b) for b in range(2)]
         v_w = [held([P, BANK], I32, "v_w%d" % u) for u in range(2)]
         v_s = [held([P, BANK], U8, "v_s%d" % u) for u in range(2)]
         page = held([P, T2], F32, "page")
         ident = held([P, P], F32, "ident")
-        zero_in = keep.tile([P, 1], F32, name="zero_in", tag="tab_w", align_bytes=64)
+        zero_in = early.tile([P, 3 * S], F32, name="zero_in", offset=0)
         zero = held([P, 1], F32, "zero")
         tx = [held([P, S], F32, "tx%d" % u) for u in range(2)]
         hw = [held([P, S], F32, "hw%d" % u) for u in range(2)]
@@ -74,70 +74,71 @@ def tile_list_skirt_flutter_features_kernel(
         w1_rows = w1.rearrange("(p j) c -> p j c", j=PACK)
 
         nc.vector.memset(tab_s[:].bitcast(I32), 0)
-        nc.vector.memset(w2_raw_s[:].bitcast(I32), 0)
-        nc.gpsimd.memset(zero_in[:], 0.0)
-        nc.scalar.activation(zero[:], zero_in[:], ACT.Silu)
+        nc.vector.memset(zero_in[:, 0:1], 0.0)
+        nc.scalar.activation(zero[:], zero_in[:, 0:1], ACT.Silu)
         nc.sync.dma_start(idx[:], offs)
         nc.sync.dma_start(idx2[:], offs2)
         nc.sync.dma_start(idx3[:], offs3)
-        nc.sync.dma_start(w2_raw_w[:], w2_words[0].rearrange("p c i -> p (c i)").bitcast(I32))
-        w1_raw = [None, None]
-        w1_raw[0] = keep.tile([P, PACK, BANK], F32, name="w1_raw", tag="w1_raw", align_bytes=64)
-        nc.sync.dma_start(w1_raw[0][:], w1_rows[:, :, 0:BANK])
-        tab_w = keep.tile([P, T], I32, name="tab_w", tag="tab_w", align_bytes=64)
+        amp_t = held([P, TILES], F32, "amp_t")
+        nc.sync.dma_start(amp_t[:].rearrange("p (b i) -> p b i", b=2), amp.rearrange("(b p i) -> p b i", p=P, i=PACK))
         nc.sync.dma_start(tab_w[:], tab_words[0].rearrange("p t i -> p (t i)").bitcast(I32))
         for q in range(4):
-            nc.scalar.dma_start(tab_s[32 * q : 32 * q + 4, :].bitcast(I32), tab_scales[0, 4 * q : 4 * q + 4, :].bitcast(I32))
-        for q in range(4):
-            nc.scalar.dma_start(w2_raw_s[32 * q : 32 * q + 4, :].bitcast(I32), w2_scales[0, 4 * q : 4 * q + 4, :].bitcast(I32))
+            nc.sync.dma_start(tab_s[32 * q : 32 * q + 4, :].bitcast(I32), tab_scales[0, 4 * q : 4 * q + 4, :].bitcast(I32))
+        w1_raw = [None, None]
+        w1_raw[0] = early.tile([P, PACK, BANK], F32, name="w1_raw0", offset=0)
+        nc.sync.dma_start(w1_raw[0][:], w1_rows[:, :, 0:BANK])
         nc.vector.memset(page[:], 0.0)
+        nc.vector.memset(w2_raw_s[:].bitcast(I32), 0)
+        w2_raw_w = early.tile([P, H], I32, name="w2_raw_w", offset=8 * S)
+        nc.sync.dma_start(w2_raw_w[:], w2_words[0].rearrange("p c i -> p (c i)").bitcast(I32))
+        for q in range(4):
+            nc.sync.dma_start(w2_raw_s[32 * q : 32 * q + 4, :].bitcast(I32), w2_scales[0, 4 * q : 4 * q + 4, :].bitcast(I32))
         make_identity(nc, ident[:])
 
-        def cast_w1(engine_copy, b, i):
-            engine_copy(
-                w1_bf[b][:, BANK * i : BANK * (i + 1)].rearrange("p (m j) -> p m j", j=PACK),
-                w1_raw[b][:].rearrange("p j (m i) -> p i m j", i=PACK)[:, i],
-            )
+        def prepare_w1(b, first, count, offset):
+            staged = early.tile([P, count * BANK], BF16, name="w1_bf%d%d" % (b, first), offset=offset, align_bytes=64)
+            for pair in range(count // 2):
+                nc.scalar.copy(
+                    staged[:, 2 * BANK * pair : 2 * BANK * (pair + 1)].rearrange("p (i m j) -> p m j i", i=2, j=PACK),
+                    w1_raw[b][:].rearrange("p j (m i) -> p m j i", i=PACK)[:, :, :, first + 2 * pair : first + 2 * pair + 2],
+                )
+            cols = slice(P * first, P * (first + count))
+            nc.vector.quantize_mx(out=w1_w[b][:, cols].bitcast(FP8X4), scales=w1_s[b][:, cols], in_=staged[:])
 
-        def quantize_w1(b):
-            nc.vector.quantize_mx(out=w1_w[b][:].bitcast(FP8X4), scales=w1_s[b][:], in_=w1_bf[b][:])
+        def deal_w2(b):
+            for raw, dealt in ((w2_raw_w, w2_w), (w2_raw_s, w2_s)):
+                nc.vector.tensor_copy(
+                    dealt[:, BANK * b : BANK * (b + 1)].rearrange("p (i m) -> p m i", i=PACK),
+                    raw[:, BANK * b : BANK * (b + 1)].rearrange("p (m i) -> p m i", i=PACK),
+                )
 
-        nc.vector.tensor_copy(
-            w2_w[:].rearrange("p (b i m) -> p b i m", b=2, i=PACK), w2_raw_w[:].rearrange("p (b m i) -> p b i m", b=2, i=PACK)
-        )
-        nc.vector.tensor_copy(
-            w2_s[:].rearrange("p (b i m) -> p b i m", b=2, i=PACK), w2_raw_s[:].rearrange("p (b m i) -> p b i m", b=2, i=PACK)
-        )
-        gains = keep.tile([P, S + M + 2 * TILES], F32, name="gains", tag="gains")
-        wgs_t = gains[:, 0:S]
-        wgt_t = gains[:, S : S + M]
-        amp_t = gains[:, S + M : S + M + TILES]
-        lift_t = gains[:, S + M + TILES : S + M + 2 * TILES]
-        nc.sync.dma_start(amp_t.rearrange("p (b i) -> p b i", b=2), amp.rearrange("(b p i) -> p b i", p=P, i=PACK))
-        nc.sync.dma_start(wgs_t, wgs)
-        nc.sync.dma_start(wgt_t, wgt)
-        nc.sync.dma_start(lift_t.rearrange("p (b i) -> p b i", b=2), lift.rearrange("(b p i) -> p b i", p=P, i=PACK))
-        for i in range(PACK):
-            cast_w1(nc.vector.tensor_copy, 0, i)
-        quantize_w1(0)
-        w1_raw[1] = keep.tile([P, PACK, BANK], F32, name="w1_raw", tag="w1_raw", align_bytes=64)
-        nc.sync.dma_start(w1_raw[1][:], w1_rows[:, :, BANK : 2 * BANK])
         for u in range(2):
             part = idx[:, 32 * u : 32 * (u + 1)]
             nc.vector.tensor_copy(v_w[u][:].bitcast(U32), tab_w[:].bitcast(U32).indirect(part))
             nc.vector.tensor_copy(v_s[u][:], tab_s[:].indirect(part))
+        wgs_t = early.tile([P, S], F32, name="wgs_t", offset=13 * S)
+        wgt_t = early.tile([P, M], F32, name="wgt_t", offset=17 * S)
+        w1_raw[1] = early.tile([P, PACK, BANK], F32, name="w1_raw1", offset=21 * S)
+        nc.sync.dma_start(wgs_t[:], wgs)
+        nc.sync.dma_start(w1_raw[1][:], w1_rows[:, :, BANK : 2 * BANK])
+        nc.sync.dma_start(wgt_t[:], wgt)
+        prepare_w1(0, 0, 2, 29 * S)
+        deal_w2(0)
 
         def half(u):
             return slice(BANK * u, BANK * (u + 1))
 
         linear = {}
 
+        def bent_of(t):
+            return xm if t == 1 else tx[t % 2]
+
         def products(t):
             b, i = divmod(t, PACK)
             cols = slice(P * i, P * (i + 1))
             cols2 = slice(P * t, P * (t + 1))
             for u in range(2):
-                bent = banks[u]
+                bent = banks[2 + u] if t == 1 else banks[u]
                 nc.tensor.matmul_mx(
                     out=bent[:], lhsT=w1_w[b][:, cols].bitcast(FP8X4), lhsT_scale=w1_s[b][:, cols],
                     rhs=v_w[u][:].bitcast(FP8X4), rhs_scale=v_s[u][:], start=True, stop=True,
@@ -148,17 +149,17 @@ def tile_list_skirt_flutter_features_kernel(
                     rhs=v_w[u][:].bitcast(FP8X4), rhs_scale=v_s[u][:], start=True, stop=True,
                 )
                 linear[t, u] = lin
-                nc.scalar.activation(tx[t % 2][:, half(u)], bent[:], ACT.Tanh, bias=zero[:])
+                nc.scalar.activation(bent_of(t)[:, half(u)], bent[:], ACT.Tanh, bias=zero[:])
 
         h_of = {}
 
         def difference(t):
             b, i = divmod(t, PACK)
-            diff = tx[(t + 1) % 2]
+            diff = tx[(t + 1) % 2] if t else early.tile([P, 2 * S], F32, name="diff0", offset=31 * S)
             h = hw[t % 2]
             for u in range(2):
                 nc.vector.scalar_tensor_tensor(
-                    diff[:, half(u)], tx[t % 2][:, half(u)], amp_t[:, t : t + 1], linear[t, u][:], ALU.mult, ALU.subtract
+                    diff[:, half(u)], bent_of(t)[:, half(u)], amp_t[:, t : t + 1], linear[t, u][:], ALU.mult, ALU.subtract
                 )
                 if t == 0:
                     nc.scalar.activation(h[:, half(u)], diff[:, half(u)], ACT.Abs)
@@ -173,10 +174,10 @@ def tile_list_skirt_flutter_features_kernel(
                         page[:].indirect(idx2[:, 32 * u : 32 * (u + 1)]), h_of[t][:, half(u)], wgs_t[:, half(u)], ALU.mult
                     )
             else:
-                nc.vector.tensor_tensor(page[:].indirect(idx2[:]), h_of[t][:], wgs_t, ALU.mult)
+                nc.vector.tensor_tensor(page[:].indirect(idx2[:]), h_of[t][:], wgs_t[:], ALU.mult)
 
         def pick(t):
-            nc.vector.tensor_tensor(xm[:], page[:].indirect(idx3[:]), wgt_t, ALU.mult)
+            nc.vector.tensor_tensor(xm[:], page[:].indirect(idx3[:]), wgt_t[:], ALU.mult)
 
         swell_of = {}
 
@@ -225,14 +226,23 @@ def tile_list_skirt_flutter_features_kernel(
             nc.vector.quantize_mx(out=z_w[b][:, cols].bitcast(FP8X4), scales=z_s[b][:, cols], in_=woven)
 
         last = TILES - 1
-        load_swell(0)
         products(0)
+        deal_w2(1)
         difference(0)
-        extras = {1: [0, 1, 2], 2: [3]}
+        load_swell(0)
+        late = early.tile([P, M + TILES], F32, name="late", offset=8 * S)
+        swell_last = late[:, 0:M]
+        lift_t = late[:, M : M + TILES]
+        nc.sync.dma_start(swell_last, swell_rows[1, PACK - 1])
+        nc.sync.dma_start(lift_t.rearrange("p (b i) -> p b i", b=2), lift.rearrange("(b p i) -> p b i", p=P, i=PACK))
         swell_turns = held([P, M], F32, "swell_turns")
         for t in range(1, TILES + 1):
             if t < TILES:
                 products(t)
+            if t == 1:
+                prepare_w1(0, 2, 2, 31 * S)
+                prepare_w1(1, 0, PACK, 33 * S)
+                nc.scalar.activation(swell_turns[:], swell_last, ACT.Copy, scale=1.0 / TURN)
             if t >= 2:
                 sine(t - 2)
             if 2 <= t <= last:
@@ -249,29 +259,22 @@ def tile_list_skirt_flutter_features_kernel(
             if t < TILES:
                 pick(t - 1)
             if t == 1:
-                w3_w = keep.tile([P, 2, 2 * N], U8, name="w3_w", tag="w1_bf0", align_bytes=64)
+                w3_w = early.tile([P, 2, 2 * N], U8, name="w3_w", offset=4 * S, align_bytes=64)
                 nc.sync.dma_start(w3_w[:].bitcast(I32), w3_words.bitcast(I32).rearrange("b p c -> p b c"))
-            for i in extras.get(t, []):
-                cast_w1(nc.scalar.copy, 1, i)
             if t == 2:
-                quantize_w1(1)
-                w3_s = keep.tile([P, 2 * N], U8, name="w3_s", tag="w1_raw", align_bytes=64)
+                w3_s = early.tile([P, 2 * N], U8, name="w3_s", offset=0, align_bytes=64)
                 nc.gpsimd.memset(w3_s[:].bitcast(I32), 0)
                 for q in range(4):
                     nc.sync.dma_start(
                         w3_s[32 * q : 32 * q + 4, :].bitcast(I32).rearrange("r (b c) -> r b c", b=2),
                         w3_scales[:, 4 * q : 4 * q + 4, :].bitcast(I32).rearrange("b r c -> r b c"),
                     )
-                swell_last = keep.tile([P, M], F32, name="swell_last", tag="w1_bf1", align_bytes=64)
-                nc.sync.dma_start(swell_last[:], swell_rows[1, PACK - 1])
-            if t == 3:
-                nc.scalar.activation(swell_turns[:], swell_last[:], ACT.Copy, scale=1.0 / TURN)
 
-        out_rows = out.rearrange("(g n p) m -> g p n m", p=P, n=2)
+        out_rows = out.rearrange("(n p) m -> p n m", p=P)
 
         starts = [sum(WIDTHS[:c]) for c in range(len(WIDTHS))]
         chunks = len(WIDTHS)
-        ends = [xm[:, half(0)], xm[:, half(1)], tx[1][:, half(0)], tx[1][:, half(1)]]
+        ends = [tx[1][:, half(0)], xm[:, half(0)], xm[:, half(1)]]
         small = ctx.enter_context(tc.tile_pool(name="small", bufs=DEPTH))
 
         def front(c):
@@ -292,18 +295,20 @@ def tile_list_skirt_flutter_features_kernel(
             cols = slice(starts[c], starts[c] + WIDTHS[c])
             quantize_z(1, cols, weave(nc.scalar.copy if c in WOVEN_BY_SCALAR else nc.vector.tensor_copy, 1, cols, ends[c % ENDS][:, 0 : 2 * WIDTHS[c]].bitcast(BF16)))
 
-        out_banks = [2, 3, 4, 5, 0, 1, 6, 7]
+        cycled = [banks[2 + n % 4] for n in range(12)]
+        reserved = [banks[0], banks[1], banks[6], banks[7]]
+        copies = []
 
         def back(c):
             width = WIDTHS[c]
             cols = slice(starts[c], starts[c] + width)
-            for g in range(N // (2 * P)):
-                bank = out_banks[(3 * c + g) % 8]
-                acc = banks[bank][:, 0 : 2 * width].rearrange("p (n m) -> p n m", n=2)
-                passes = (1, 0) if 4 <= 3 * c + g < 8 else (0, 1)
-                steps = [(b, n, w) for b in passes for n in range(2) for w in range(width // P)]
+            together = 2 if width == CHUNK else 3
+            for first in range(0, N // P, together):
+                bank = (cycled if cols.start < M - CHUNK else reserved).pop(0)
+                acc = bank[:, 0 : together * width].rearrange("p (n m) -> p n m", n=together)
+                steps = [(b, n, w) for b in range(2) for n in range(together) for w in range(width // P)]
                 for s, (b, n, w) in enumerate(steps):
-                    rows = 2 * g + n
+                    rows = first + n
                     part = slice(cols.start + P * w, cols.start + P * (w + 1))
                     nc.tensor.matmul_mx(
                         out=acc[:, n, P * w : P * (w + 1)],
@@ -313,17 +318,20 @@ def tile_list_skirt_flutter_features_kernel(
                         rhs_scale=z_s[b][:, part],
                         start=(s == 0), stop=(s == len(steps) - 1),
                     )
-                result = keep.tile([P, 2, width], F32, name="result%d_%d" % (c, g))
-                if (c, g) in ON_VECTOR:
+                result = keep.tile([P, together, width], F32, name="result%d_%d" % (c, first))
+                if len(copies) >= SHARED_FROM and (len(copies) - SHARED_FROM) % 2 == 0:
                     nc.vector.tensor_copy(result[:], acc)
                 else:
                     nc.scalar.copy(result[:], acc)
-                nc.sync.dma_start(out_rows[g, :, :, cols], result[:])
+                copies.append(result)
+                nc.sync.dma_start(out_rows[:, first : first + together, cols], result[:])
 
         for c in range(ENDS):
             front(c)
+        middle(0)
         for c in range(chunks):
-            middle(c)
             if c + ENDS < chunks:
                 front(c + ENDS)
+            if c + 1 < chunks:
+                middle(c + 1)
             back(c)

@@ -25,12 +25,13 @@ TILES = H // P
 TURN = 2.0 * math.pi
 ROUNDER = 1.5 * 2.0**23
 CHUNK = 256
-EARLY = {6: [0, 1], 7: [2], 8: [3]}
+PICKED = 40 * S
+EARLY = {6: slice(0, 384), 7: slice(384, 768), 8: slice(768, 1024)}
 WOVEN_BY_SCALAR = []
 ENDS = 3
 DEPTH = 1
 SHARED_FROM = 6
-WIDTHS = [256, 256, 256, 128, 128]
+WIDTHS = [256] * 4
 
 
 def tile_list_skirt_flutter_features_kernel(
@@ -59,14 +60,14 @@ def tile_list_skirt_flutter_features_kernel(
         w1_s = [held([P, BANK], U8, "w1_s%d" % b) for b in range(2)]
         v_w = [held([P, BANK], I32, "v_w%d" % u) for u in range(2)]
         v_s = [held([P, BANK], U8, "v_s%d" % u) for u in range(2)]
-        page = held([P, T2], F32, "page")
+        pages = [held([P, T2], F32, "page%d" % u) for u in range(2)]
         ident = held([P, P], F32, "ident")
         zero_in = early.tile([P, 3 * S], F32, name="zero_in", offset=0)
         zero = held([P, 1], F32, "zero")
         tx = [held([P, S], F32, "tx%d" % u) for u in range(2)]
         hw = [held([P, S], F32, "hw%d" % u) for u in range(2)]
         wave = held([P, M], F32, "wave")
-        xm = held([P, M], F32, "xm")
+        picked = {}
         z_rows = [held([P, PACK, M], BF16, "z_rows%d" % b) for b in range(2)]
         z_w = [held([P, M], I32, "z_w%d" % b) for b in range(2)]
         z_s = [held([P, M], U8, "z_s%d" % b) for b in range(2)]
@@ -87,12 +88,13 @@ def tile_list_skirt_flutter_features_kernel(
         w1_raw = [None, None]
         w1_raw[0] = early.tile([P, PACK, BANK], F32, name="w1_raw0", offset=0)
         nc.sync.dma_start(w1_raw[0][:], w1_rows[:, :, 0:BANK])
-        nc.vector.memset(page[:], 0.0)
+        nc.vector.memset(pages[0][:], 0.0)
         nc.vector.memset(w2_raw_s[:].bitcast(I32), 0)
         w2_raw_w = early.tile([P, H], I32, name="w2_raw_w", offset=8 * S)
         nc.sync.dma_start(w2_raw_w[:], w2_words[0].rearrange("p c i -> p (c i)").bitcast(I32))
         for q in range(4):
             nc.sync.dma_start(w2_raw_s[32 * q : 32 * q + 4, :].bitcast(I32), w2_scales[0, 4 * q : 4 * q + 4, :].bitcast(I32))
+        nc.vector.memset(pages[1][:], 0.0)
         make_identity(nc, ident[:])
 
         def prepare_w1(b, first, count, offset):
@@ -129,9 +131,10 @@ def tile_list_skirt_flutter_features_kernel(
             return slice(BANK * u, BANK * (u + 1))
 
         linear = {}
+        bent1 = early.tile([P, S], F32, name="bent1", offset=PICKED)
 
         def bent_of(t):
-            return xm if t == 1 else tx[t % 2]
+            return bent1 if t == 1 else tx[t % 2]
 
         def products(t):
             b, i = divmod(t, PACK)
@@ -168,6 +171,7 @@ def tile_list_skirt_flutter_features_kernel(
             h_of[t] = h
 
         def put(t):
+            page = pages[t % 2]
             if t == 0:
                 for u in range(2):
                     nc.vector.tensor_tensor(
@@ -177,7 +181,8 @@ def tile_list_skirt_flutter_features_kernel(
                 nc.vector.tensor_tensor(page[:].indirect(idx2[:]), h_of[t][:], wgs_t[:], ALU.mult)
 
         def pick(t):
-            nc.vector.tensor_tensor(xm[:], page[:].indirect(idx3[:]), wgt_t[:], ALU.mult)
+            picked[t] = early.tile([P, M], F32, name="picked%d" % t, offset=PICKED)
+            nc.vector.tensor_tensor(picked[t][:], pages[t % 2][:].indirect(idx3[:]), wgt_t[:], ALU.mult)
 
         swell_of = {}
 
@@ -196,24 +201,28 @@ def tile_list_skirt_flutter_features_kernel(
 
         def sine(t):
             b, i = divmod(t, PACK)
-            x = xm
+            x = picked[t]
             turns = tx[(t + 1) % 2]
-            minus = xm
             pair = banks[2 + 2 * ((t + 1) % 2) :]
             for u in range(2):
-                add_turned(pair[u], [x[:, half(u)], swell_of[t][:, half(u)]])
+                add_turned(pair[u], [swell_of[t][:, half(u)], x[:, half(u)]])
             for u in range(2):
                 nc.scalar.activation(turns[:, half(u)], pair[u][:], ACT.Copy, scale=1.0 / TURN)
-                whole = keep.tile([P, BANK], U32, name="whole", tag="whole%d%d" % (t % 2, u), align_bytes=64)
+                if u == 0:
+                    whole = keep.tile([P, BANK], U32, name="whole", tag="whole%d" % (t % 2), align_bytes=64)
+                else:
+                    whole = early.tile([P, BANK], U32, name="whole%d" % t, offset=PICKED)
+                minus = keep.tile([P, BANK], F32, name="minus", tag="minus%d" % u, align_bytes=64)
                 nc.scalar.activation(whole[:], turns[:, half(u)], ACT.Copy, bias=ROUNDER)
-                nc.scalar.activation(minus[:, half(u)], whole[:], ACT.Copy, scale=-1.0, bias=ROUNDER)
-                add_turned(pair[u], [turns[:, half(u)], minus[:, half(u)]])
-            for u in range(2):
-                nc.scalar.activation(wave[:, half(u)], pair[u][:], ACT.Sin, scale=TURN)
+                nc.scalar.activation(minus[:], whole[:], ACT.Copy, scale=-1.0, bias=ROUNDER)
+                add_turned(pair[u], [turns[:, half(u)], minus[:]])
 
         def gain(t):
             b, i = divmod(t, PACK)
-            nc.scalar.activation(z_rows[b][:, i, :], wave[:], ACT.Copy, scale=lift_t[:, t : t + 1])
+            pair = banks[2 + 2 * ((t + 1) % 2) :]
+            for u in range(2):
+                nc.scalar.activation(wave[:, half(u)], pair[u][:], ACT.Sin, scale=TURN)
+                nc.scalar.activation(z_rows[b][:, i, half(u)], wave[:, half(u)], ACT.Copy, scale=lift_t[:, t : t + 1])
 
         def weave(engine_copy, b, cols, woven):
             engine_copy(
@@ -224,6 +233,13 @@ def tile_list_skirt_flutter_features_kernel(
 
         def quantize_z(b, cols, woven):
             nc.vector.quantize_mx(out=z_w[b][:, cols].bitcast(FP8X4), scales=z_s[b][:, cols], in_=woven)
+
+        def weave_early(cols, tag):
+            woven = keep.tile([P, (cols.stop - cols.start) * PACK], BF16, name="woven", tag=tag, align_bytes=64)
+            weave(nc.scalar.copy, 0, cols, woven[:])
+            for first in range(cols.start, cols.stop, CHUNK):
+                part = slice(first, min(first + CHUNK, cols.stop))
+                quantize_z(0, part, woven[:, PACK * (part.start - cols.start) : PACK * (part.stop - cols.start)])
 
         last = TILES - 1
         products(0)
@@ -248,10 +264,8 @@ def tile_list_skirt_flutter_features_kernel(
             if 2 <= t <= last:
                 load_swell(t - 1)
             put(t - 1)
-            for u, c in enumerate(EARLY.get(t, [])):
-                cols = slice(CHUNK * c, CHUNK * (c + 1))
-                woven = keep.tile([P, CHUNK * PACK], BF16, name="woven", tag="whole%d%d" % (t % 2, u), align_bytes=64)
-                quantize_z(0, cols, weave(nc.scalar.copy, 0, cols, woven[:]))
+            if t in EARLY:
+                weave_early(EARLY[t], "whole%d" % (t % 2))
             if t < TILES:
                 difference(t)
             if t >= 2:
@@ -274,7 +288,8 @@ def tile_list_skirt_flutter_features_kernel(
 
         starts = [sum(WIDTHS[:c]) for c in range(len(WIDTHS))]
         chunks = len(WIDTHS)
-        ends = [tx[1][:, half(0)], xm[:, half(0)], xm[:, half(1)]]
+        both = early.tile([P, M], F32, name="ends", offset=PICKED, align_bytes=64)
+        ends = [tx[1][:, half(0)], both[:, half(0)], both[:, half(1)]]
         small = ctx.enter_context(tc.tile_pool(name="small", bufs=DEPTH))
 
         def front(c):
@@ -284,7 +299,7 @@ def tile_list_skirt_flutter_features_kernel(
             turns = small.tile([P, width], F32, name="turns_end")
             whole = small.tile([P, width], I32, name="whole_end")
             rest = small.tile([P, width], F32, name="rest_end")
-            nc.vector.tensor_tensor(x, page[:].indirect(idx3[:, cols.start // 16 : cols.stop // 16]), wgt_t[:, cols], ALU.mult)
+            nc.vector.tensor_tensor(x, pages[last % 2][:].indirect(idx3[:, cols.start // 16 : cols.stop // 16]), wgt_t[:, cols], ALU.mult)
             nc.vector.scalar_tensor_tensor(turns[:], x, 1.0 / TURN, swell_turns[:, cols], ALU.mult, ALU.add)
             nc.vector.tensor_scalar(whole[:], turns[:], ROUNDER, None, ALU.add)
             nc.vector.scalar_tensor_tensor(rest[:], whole[:], ROUNDER, turns[:], ALU.subtract, ALU.subtract)

@@ -27,10 +27,10 @@ ROUNDER = 1.5 * 2.0**23
 CHUNK = 256
 PICKED = 40 * S
 EARLY = {6: slice(0, 384), 7: slice(384, 768), 8: slice(768, 1024)}
-WOVEN_BY_SCALAR = []
-ENDS = 3
-DEPTH = 1
-SHARED_FROM = 6
+WOVEN_BY_SCALAR = [0, 1]
+ORDER = [2, 3, 4, 5, 2, 3, 0, 1, 6, 7, 4, 5]
+DEPTH = 2
+SHARED_FROM = 3
 WIDTHS = [256] * 4
 
 
@@ -289,64 +289,61 @@ def tile_list_skirt_flutter_features_kernel(
         starts = [sum(WIDTHS[:c]) for c in range(len(WIDTHS))]
         chunks = len(WIDTHS)
         both = early.tile([P, M], F32, name="ends", offset=PICKED, align_bytes=64)
-        ends = [tx[1][:, half(0)], both[:, half(0)], both[:, half(1)]]
+        ends = [tx[1][:, half(0)], tx[1][:, half(1)], both[:, half(0)], both[:, half(1)]]
         small = ctx.enter_context(tc.tile_pool(name="small", bufs=DEPTH))
 
-        def front(c):
-            width = WIDTHS[c]
-            cols = slice(starts[c], starts[c] + width)
-            x = ends[c % ENDS][:, 0:width]
+        rest = held([P, M], F32, "rest")
+
+        def reduce_last(cols, x, rest):
+            width = cols.stop - cols.start
             turns = small.tile([P, width], F32, name="turns_end")
             whole = small.tile([P, width], I32, name="whole_end")
-            rest = small.tile([P, width], F32, name="rest_end")
             nc.vector.tensor_tensor(x, pages[last % 2][:].indirect(idx3[:, cols.start // 16 : cols.stop // 16]), wgt_t[:, cols], ALU.mult)
             nc.vector.scalar_tensor_tensor(turns[:], x, 1.0 / TURN, swell_turns[:, cols], ALU.mult, ALU.add)
             nc.vector.tensor_scalar(whole[:], turns[:], ROUNDER, None, ALU.add)
-            nc.vector.scalar_tensor_tensor(rest[:], whole[:], ROUNDER, turns[:], ALU.subtract, ALU.subtract)
-            nc.scalar.activation(wave[:, cols], rest[:], ACT.Sin, scale=-TURN)
+            nc.vector.scalar_tensor_tensor(rest[:, cols], whole[:], ROUNDER, turns[:], ALU.subtract, ALU.subtract)
+
+        def front(c, rest):
+            cols = slice(starts[c], starts[c] + WIDTHS[c])
+            nc.scalar.activation(wave[:, cols], rest[:, cols], ACT.Sin, scale=-TURN)
             nc.scalar.activation(z_rows[1][:, PACK - 1, cols], wave[:, cols], ACT.Copy, scale=lift_t[:, last : last + 1])
 
-        def middle(c):
-            cols = slice(starts[c], starts[c] + WIDTHS[c])
-            quantize_z(1, cols, weave(nc.scalar.copy if c in WOVEN_BY_SCALAR else nc.vector.tensor_copy, 1, cols, ends[c % ENDS][:, 0 : 2 * WIDTHS[c]].bitcast(BF16)))
+        def middle(u):
+            woven = (tx[1], both)[u][:].bitcast(BF16)
+            for c in range(2):
+                cols = slice(BANK * u + CHUNK * c, BANK * u + CHUNK * (c + 1))
+                weave(nc.scalar.copy if 2 * u + c in WOVEN_BY_SCALAR else nc.vector.tensor_copy, 1, cols, woven[:, PACK * CHUNK * c : PACK * CHUNK * (c + 1)])
+            quantize_z(1, half(u), woven)
 
-        cycled = [banks[2 + n % 4] for n in range(12)]
-        reserved = [banks[0], banks[1], banks[6], banks[7]]
-        copies = []
+        out_banks = ORDER
 
-        def back(c):
-            width = WIDTHS[c]
-            cols = slice(starts[c], starts[c] + width)
-            together = 2 if width == CHUNK else 3
-            for first in range(0, N // P, together):
-                bank = (cycled if cols.start < M - CHUNK else reserved).pop(0)
-                acc = bank[:, 0 : together * width].rearrange("p (n m) -> p n m", n=together)
-                steps = [(b, n, w) for b in range(2) for n in range(together) for w in range(width // P)]
-                for s, (b, n, w) in enumerate(steps):
-                    rows = first + n
-                    part = slice(cols.start + P * w, cols.start + P * (w + 1))
+        def back(u):
+            for rows in range(N // P):
+                n = (N // P) * u + rows
+                acc = banks[out_banks[n]]
+                for b in range(2):
                     nc.tensor.matmul_mx(
-                        out=acc[:, n, P * w : P * (w + 1)],
+                        out=acc[:],
                         lhsT=w3_w[:, b, 2 * P * rows : 2 * P * (rows + 1)].bitcast(FP4X4),
                         lhsT_scale=w3_s[:, N * b + P * rows : N * b + P * (rows + 1)],
-                        rhs=z_w[b][:, part].bitcast(FP8X4),
-                        rhs_scale=z_s[b][:, part],
-                        start=(s == 0), stop=(s == len(steps) - 1),
+                        rhs=z_w[b][:, half(u)].bitcast(FP8X4),
+                        rhs_scale=z_s[b][:, half(u)],
+                        start=(b == 0), stop=(b == 1),
                     )
-                result = keep.tile([P, together, width], F32, name="result%d_%d" % (c, first))
-                if len(copies) >= SHARED_FROM and (len(copies) - SHARED_FROM) % 2 == 0:
-                    nc.vector.tensor_copy(result[:], acc)
+                result = keep.tile([P, BANK], F32, name="result%d" % n)
+                if n >= SHARED_FROM and (n - SHARED_FROM) % 2 == 0:
+                    nc.vector.tensor_copy(result[:], acc[:])
                 else:
-                    nc.scalar.copy(result[:], acc)
-                copies.append(result)
-                nc.sync.dma_start(out_rows[:, first : first + together, cols], result[:])
+                    nc.scalar.copy(result[:], acc[:])
+                nc.sync.dma_start(out_rows[:, rows, half(u)], result[:])
 
-        for c in range(ENDS):
-            front(c)
+        for c in range(2):
+            reduce_last(slice(CHUNK * c, CHUNK * (c + 1)), tx[1][:, BANK * c : BANK * c + CHUNK], rest)
+            front(c, rest)
         middle(0)
-        for c in range(chunks):
-            if c + ENDS < chunks:
-                front(c + ENDS)
-            if c + 1 < chunks:
-                middle(c + 1)
-            back(c)
+        reduce_last(half(1), rest[:, half(0)], rest)
+        front(2, rest)
+        front(3, rest)
+        middle(1)
+        back(0)
+        back(1)

import math
from contextlib import ExitStack

import concourse.mybir as mybir
from concourse.masks import make_identity

K, T, S, T2, M, H, N = 512, 4096, 1024, 2048, 1024, 1024, 768
FLOPS = 2 * (2 * K * H * S + H * N * M)

F32 = mybir.dt.float32
BF16 = mybir.dt.bfloat16
I32 = mybir.dt.int32
U32 = mybir.dt.uint32
U16 = mybir.dt.uint16
U8 = mybir.dt.uint8
FP8X4 = mybir.dt.float8_e4m3fn_x4
FP4X4 = mybir.dt.float4_e2m1fn_x4
ACT = mybir.ActivationFunctionType
ALU = mybir.AluOpType

P = 128
PACK = 4
BANK = 512
TILES = H // P
TURN = 2.0 * math.pi
ROUNDER = 1.5 * 2.0**23
CHUNK = 256
PICKED = 40 * S
EARLY = {6: slice(0, 384), 7: slice(384, 768), 8: slice(768, 1024)}
WOVEN_BY_SCALAR = [0, 1]
ORDER = [2, 3, 4, 5, 2, 3, 0, 1, 6, 7, 4, 5]
DEPTH = 2
SHARED_FROM = 3
WIDTHS = [256] * 4


def tile_list_skirt_flutter_features_kernel(
    tc, tab_words, tab_scales, offs, offs2, offs3, wgs, wgt, w1, w2_words, w2_scales, amp, swell, lift, w3_words, w3_scales, out
):
    nc = tc.nc
    with ExitStack() as ctx:
        keep = ctx.enter_context(tc.tile_pool(name="keep", bufs=1))
        ring = ctx.enter_context(tc.tile_pool(name="ring", bufs=2))
        early = ctx.enter_context(tc.tile_pool(name="early", bufs=1))
        psum = ctx.enter_context(tc.psum_pool(name="psum", bufs=1))
        banks = [psum.tile([P, BANK], F32, name="bank%d" % n) for n in range(8)]

        def held(shape, dtype, name):
            return keep.tile(shape, dtype, name=name, align_bytes=64)

        idx = held([P, S // 16], U16, "idx")
        idx2 = held([P, S // 16], U16, "idx2")
        idx3 = held([P, M // 16], U16, "idx3")
        tab_w = early.tile([P, T], I32, name="tab_w", offset=13 * S)
        tab_s = held([P, T], U8, "tab_s")
        w2_raw_s = keep.tile([P, H], U8, name="w2_raw_s", tag="rows")
        w2_w = held([P, H], I32, "w2_w")
        w2_s = held([P, H], U8, "w2_s")
        w1_w = [held([P, BANK], I32, "w1_w%d" % b) for b in range(2)]
        w1_s = [held([P, BANK], U8, "w1_s%d" % b) for b in range(2)]
        v_w = [held([P, BANK], I32, "v_w%d" % u) for u in range(2)]
        v_s = [held([P, BANK], U8, "v_s%d" % u) for u in range(2)]
        pages = [held([P, T2], F32, "page%d" % u) for u in range(2)]
        ident = held([P, P], F32, "ident")
        zero_in = early.tile([P, 3 * S], F32, name="zero_in", offset=0)
        zero = held([P, 1], F32, "zero")
        tx = [held([P, S], F32, "tx%d" % u) for u in range(2)]
        hw = [held([P, S], F32, "hw%d" % u) for u in range(2)]
        wave = held([P, M], F32, "wave")
        picked = {}
        z_rows = [held([P, PACK, M], BF16, "z_rows%d" % b) for b in range(2)]
        z_w = [held([P, M], I32, "z_w%d" % b) for b in range(2)]
        z_s = [held([P, M], U8, "z_s%d" % b) for b in range(2)]
        swell_rows = swell.rearrange("(b p i) m -> b i p m", p=P, i=PACK)
        w1_rows = w1.rearrange("(p j) c -> p j c", j=PACK)

        nc.vector.memset(tab_s[:].bitcast(I32), 0)
        nc.vector.memset(zero_in[:, 0:1], 0.0)
        nc.scalar.activation(zero[:], zero_in[:, 0:1], ACT.Silu)
        nc.sync.dma_start(idx[:], offs)
        nc.sync.dma_start(idx2[:], offs2)
        nc.sync.dma_start(idx3[:], offs3)
        amp_t = held([P, TILES], F32, "amp_t")
        nc.sync.dma_start(amp_t[:].rearrange("p (b i) -> p b i", b=2), amp.rearrange("(b p i) -> p b i", p=P, i=PACK))
        nc.sync.dma_start(tab_w[:], tab_words[0].rearrange("p t i -> p (t i)").bitcast(I32))
        for q in range(4):
            nc.sync.dma_start(tab_s[32 * q : 32 * q + 4, :].bitcast(I32), tab_scales[0, 4 * q : 4 * q + 4, :].bitcast(I32))
        w1_raw = [None, None]
        w1_raw[0] = early.tile([P, PACK, BANK], F32, name="w1_raw0", offset=0)
        nc.sync.dma_start(w1_raw[0][:], w1_rows[:, :, 0:BANK])
        nc.vector.memset(pages[0][:], 0.0)
        nc.vector.memset(w2_raw_s[:].bitcast(I32), 0)
        w2_raw_w = early.tile([P, H], I32, name="w2_raw_w", offset=8 * S)
        nc.sync.dma_start(w2_raw_w[:], w2_words[0].rearrange("p c i -> p (c i)").bitcast(I32))
        for q in range(4):
            nc.sync.dma_start(w2_raw_s[32 * q : 32 * q + 4, :].bitcast(I32), w2_scales[0, 4 * q : 4 * q + 4, :].bitcast(I32))
        nc.vector.memset(pages[1][:], 0.0)
        make_identity(nc, ident[:])

        def prepare_w1(b, first, count, offset):
            staged = early.tile([P, count * BANK], BF16, name="w1_bf%d%d" % (b, first), offset=offset, align_bytes=64)
            for pair in range(count // 2):
                nc.scalar.copy(
                    staged[:, 2 * BANK * pair : 2 * BANK * (pair + 1)].rearrange("p (i m j) -> p m j i", i=2, j=PACK),
                    w1_raw[b][:].rearrange("p j (m i) -> p m j i", i=PACK)[:, :, :, first + 2 * pair : first + 2 * pair + 2],
                )
            cols = slice(P * first, P * (first + count))
            nc.vector.quantize_mx(out=w1_w[b][:, cols].bitcast(FP8X4), scales=w1_s[b][:, cols], in_=staged[:])

        def deal_w2(b):
            for raw, dealt in ((w2_raw_w, w2_w), (w2_raw_s, w2_s)):
                nc.vector.tensor_copy(
                    dealt[:, BANK * b : BANK * (b + 1)].rearrange("p (i m) -> p m i", i=PACK),
                    raw[:, BANK * b : BANK * (b + 1)].rearrange("p (m i) -> p m i", i=PACK),
                )

        for u in range(2):
            part = idx[:, 32 * u : 32 * (u + 1)]
            nc.vector.tensor_copy(v_w[u][:].bitcast(U32), tab_w[:].bitcast(U32).indirect(part))
            nc.vector.tensor_copy(v_s[u][:], tab_s[:].indirect(part))
        wgs_t = early.tile([P, S], F32, name="wgs_t", offset=13 * S)
        wgt_t = early.tile([P, M], F32, name="wgt_t", offset=17 * S)
        w1_raw[1] = early.tile([P, PACK, BANK], F32, name="w1_raw1", offset=21 * S)
        nc.sync.dma_start(wgs_t[:], wgs)
        nc.sync.dma_start(w1_raw[1][:], w1_rows[:, :, BANK : 2 * BANK])
        nc.sync.dma_start(wgt_t[:], wgt)
        prepare_w1(0, 0, 2, 29 * S)
        deal_w2(0)

        def half(u):
            return slice(BANK * u, BANK * (u + 1))

        linear = {}
        bent1 = early.tile([P, S], F32, name="bent1", offset=PICKED)

        def bent_of(t):
            return bent1 if t == 1 else tx[t % 2]

        def products(t):
            b, i = divmod(t, PACK)
            cols = slice(P * i, P * (i + 1))
            cols2 = slice(P * t, P * (t + 1))
            for u in range(2):
                bent = banks[2 + u] if t == 1 else banks[u]
                nc.tensor.matmul_mx(
                    out=bent[:], lhsT=w1_w[b][:, cols].bitcast(FP8X4), lhsT_scale=w1_s[b][:, cols],
                    rhs=v_w[u][:].bitcast(FP8X4), rhs_scale=v_s[u][:], start=True, stop=True,
                )
                lin = banks[2 + 2 * (t % 2) + u]
                nc.tensor.matmul_mx(
                    out=lin[:], lhsT=w2_w[:, cols2].bitcast(FP8X4), lhsT_scale=w2_s[:, cols2],
                    rhs=v_w[u][:].bitcast(FP8X4), rhs_scale=v_s[u][:], start=True, stop=True,
                )
                linear[t, u] = lin
                nc.scalar.activation(bent_of(t)[:, half(u)], bent[:], ACT.Tanh, bias=zero[:])

        h_of = {}

        def difference(t):
            b, i = divmod(t, PACK)
            diff = tx[(t + 1) % 2] if t else early.tile([P, 2 * S], F32, name="diff0", offset=31 * S)
            h = hw[t % 2]
            for u in range(2):
                nc.vector.scalar_tensor_tensor(
                    diff[:, half(u)], bent_of(t)[:, half(u)], amp_t[:, t : t + 1], linear[t, u][:], ALU.mult, ALU.subtract
                )
                if t == 0:
                    nc.scalar.activation(h[:, half(u)], diff[:, half(u)], ACT.Abs)
            if t > 0:
                nc.scalar.activation(h[:], diff[:], ACT.Abs)
            h_of[t] = h

        def put(t):
            page = pages[t % 2]
            if t == 0:
                for u in range(2):
                    nc.vector.tensor_tensor(
                        page[:].indirect(idx2[:, 32 * u : 32 * (u + 1)]), h_of[t][:, half(u)], wgs_t[:, half(u)], ALU.mult
                    )
            else:
                nc.vector.tensor_tensor(page[:].indirect(idx2[:]), h_of[t][:], wgs_t[:], ALU.mult)

        def pick(t):
            picked[t] = early.tile([P, M], F32, name="picked%d" % t, offset=PICKED)
            nc.vector.tensor_tensor(picked[t][:], pages[t % 2][:].indirect(idx3[:]), wgt_t[:], ALU.mult)

        swell_of = {}

        def load_swell(t):
            rows = keep.tile([P, M], F32, name="swell_t", tag="rows")
            nc.sync.dma_start(rows[:], swell_rows[t // PACK, t % PACK])
            swell_of[t] = rows

        def add_turned(bank, sources):
            steps = [(src, c) for src in sources for c in range(BANK // P)]
            for n, (src, c) in enumerate(steps):
                nc.tensor.matmul(
                    bank[:, P * c : P * (c + 1)], lhsT=src[:, P * c : P * (c + 1)], rhs=ident[:],
                    is_transpose=True, start=(n == 0), stop=(n == len(steps) - 1),
                )

        def sine(t):
            b, i = divmod(t, PACK)
            x = picked[t]
            turns = tx[(t + 1) % 2]
            pair = banks[2 + 2 * ((t + 1) % 2) :]
            for u in range(2):
                add_turned(pair[u], [swell_of[t][:, half(u)], x[:, half(u)]])
            for u in range(2):
                nc.scalar.activation(turns[:, half(u)], pair[u][:], ACT.Copy, scale=1.0 / TURN)
                if u == 0:
                    whole = keep.tile([P, BANK], U32, name="whole", tag="whole%d" % (t % 2), align_bytes=64)
                else:
                    whole = early.tile([P, BANK], U32, name="whole%d" % t, offset=PICKED)
                minus = keep.tile([P, BANK], F32, name="minus", tag="minus%d" % u, align_bytes=64)
                nc.scalar.activation(whole[:], turns[:, half(u)], ACT.Copy, bias=ROUNDER)
                nc.scalar.activation(minus[:], whole[:], ACT.Copy, scale=-1.0, bias=ROUNDER)
                add_turned(pair[u], [turns[:, half(u)], minus[:]])

        def gain(t):
            b, i = divmod(t, PACK)
            pair = banks[2 + 2 * ((t + 1) % 2) :]
            for u in range(2):
                nc.scalar.activation(wave[:, half(u)], pair[u][:], ACT.Sin, scale=TURN)
                nc.scalar.activation(z_rows[b][:, i, half(u)], wave[:, half(u)], ACT.Copy, scale=lift_t[:, t : t + 1])

        def weave(engine_copy, b, cols, woven):
            engine_copy(
                woven.rearrange("p (g e i) -> p g i e", e=4, i=PACK),
                z_rows[b][:, :, cols].rearrange("p i (g e) -> p g i e", e=4),
            )
            return woven

        def quantize_z(b, cols, woven):
            nc.vector.quantize_mx(out=z_w[b][:, cols].bitcast(FP8X4), scales=z_s[b][:, cols], in_=woven)

        def weave_early(cols, tag):
            woven = keep.tile([P, (cols.stop - cols.start) * PACK], BF16, name="woven", tag=tag, align_bytes=64)
            weave(nc.scalar.copy, 0, cols, woven[:])
            for first in range(cols.start, cols.stop, CHUNK):
                part = slice(first, min(first + CHUNK, cols.stop))
                quantize_z(0, part, woven[:, PACK * (part.start - cols.start) : PACK * (part.stop - cols.start)])

        last = TILES - 1
        products(0)
        deal_w2(1)
        difference(0)
        load_swell(0)
        late = early.tile([P, M + TILES], F32, name="late", offset=8 * S)
        swell_last = late[:, 0:M]
        lift_t = late[:, M : M + TILES]
        nc.sync.dma_start(swell_last, swell_rows[1, PACK - 1])
        nc.sync.dma_start(lift_t.rearrange("p (b i) -> p b i", b=2), lift.rearrange("(b p i) -> p b i", p=P, i=PACK))
        swell_turns = held([P, M], F32, "swell_turns")
        for t in range(1, TILES + 1):
            if t < TILES:
                products(t)
            if t == 1:
                prepare_w1(0, 2, 2, 31 * S)
                prepare_w1(1, 0, PACK, 33 * S)
                nc.scalar.activation(swell_turns[:], swell_last, ACT.Copy, scale=1.0 / TURN)
            if t >= 2:
                sine(t - 2)
            if 2 <= t <= last:
                load_swell(t - 1)
            put(t - 1)
            if t in EARLY:
                weave_early(EARLY[t], "whole%d" % (t % 2))
            if t < TILES:
                difference(t)
            if t >= 2:
                gain(t - 2)
            if t < TILES:
                pick(t - 1)
            if t == 1:
                w3_w = early.tile([P, 2, 2 * N], U8, name="w3_w", offset=4 * S, align_bytes=64)
                nc.sync.dma_start(w3_w[:].bitcast(I32), w3_words.bitcast(I32).rearrange("b p c -> p b c"))
            if t == 2:
                w3_s = early.tile([P, 2 * N], U8, name="w3_s", offset=0, align_bytes=64)
                nc.gpsimd.memset(w3_s[:].bitcast(I32), 0)
                for q in range(4):
                    nc.sync.dma_start(
                        w3_s[32 * q : 32 * q + 4, :].bitcast(I32).rearrange("r (b c) -> r b c", b=2),
                        w3_scales[:, 4 * q : 4 * q + 4, :].bitcast(I32).rearrange("b r c -> r b c"),
                    )

        out_rows = out.rearrange("(n p) m -> p n m", p=P)

        starts = [sum(WIDTHS[:c]) for c in range(len(WIDTHS))]
        chunks = len(WIDTHS)
        both = early.tile([P, M], F32, name="ends", offset=PICKED, align_bytes=64)
        ends = [tx[1][:, half(0)], tx[1][:, half(1)], both[:, half(0)], both[:, half(1)]]
        small = ctx.enter_context(tc.tile_pool(name="small", bufs=DEPTH))

        rest = held([P, M], F32, "rest")

        def reduce_last(cols, x, rest):
            width = cols.stop - cols.start
            turns = small.tile([P, width], F32, name="turns_end")
            whole = small.tile([P, width], I32, name="whole_end")
            nc.vector.tensor_tensor(x, pages[last % 2][:].indirect(idx3[:, cols.start // 16 : cols.stop // 16]), wgt_t[:, cols], ALU.mult)
            nc.vector.scalar_tensor_tensor(turns[:], x, 1.0 / TURN, swell_turns[:, cols], ALU.mult, ALU.add)
            nc.vector.tensor_scalar(whole[:], turns[:], ROUNDER, None, ALU.add)
            nc.vector.scalar_tensor_tensor(rest[:, cols], whole[:], ROUNDER, turns[:], ALU.subtract, ALU.subtract)

        def front(c, rest):
            cols = slice(starts[c], starts[c] + WIDTHS[c])
            nc.scalar.activation(wave[:, cols], rest[:, cols], ACT.Sin, scale=-TURN)
            nc.scalar.activation(z_rows[1][:, PACK - 1, cols], wave[:, cols], ACT.Copy, scale=lift_t[:, last : last + 1])

        def middle(u):
            woven = (tx[1], both)[u][:].bitcast(BF16)
            for c in range(2):
                cols = slice(BANK * u + CHUNK * c, BANK * u + CHUNK * (c + 1))
                weave(nc.scalar.copy if 2 * u + c in WOVEN_BY_SCALAR else nc.vector.tensor_copy, 1, cols, woven[:, PACK * CHUNK * c : PACK * CHUNK * (c + 1)])
            quantize_z(1, half(u), woven)

        out_banks = ORDER

        def back(u):
            for rows in range(N // P):
                n = (N // P) * u + rows
                acc = banks[out_banks[n]]
                for b in range(2):
                    nc.tensor.matmul_mx(
                        out=acc[:],
                        lhsT=w3_w[:, b, 2 * P * rows : 2 * P * (rows + 1)].bitcast(FP4X4),
                        lhsT_scale=w3_s[:, N * b + P * rows : N * b + P * (rows + 1)],
                        rhs=z_w[b][:, half(u)].bitcast(FP8X4),
                        rhs_scale=z_s[b][:, half(u)],
                        start=(b == 0), stop=(b == 1),
                    )
                result = keep.tile([P, BANK], F32, name="result%d" % n)
                if n >= SHARED_FROM and (n - SHARED_FROM) % 2 == 0:
                    nc.vector.tensor_copy(result[:], acc[:])
                else:
                    nc.scalar.copy(result[:], acc[:])
                nc.sync.dma_start(out_rows[:, rows, half(u)], result[:])

        for c in range(2):
            reduce_last(slice(CHUNK * c, CHUNK * (c + 1)), tx[1][:, BANK * c : BANK * c + CHUNK], rest)
            front(c, rest)
        middle(0)
        reduce_last(half(1), rest[:, half(0)], rest)
        front(2, rest)
        front(3, rest)
        middle(1)
        back(0)
        back(1)
